import numpy as np
import ml_dtypes

BF16 = ml_dtypes.bfloat16


def bf(x):
    return np.asarray(x, np.float32).astype(BF16)


def f32(x):
    return np.asarray(x, np.float32)


def f64(x):
    return np.asarray(x).astype(np.float64)


def striped(idx):
    return np.tile(idx.reshape(-1, 16).T, (8, 1))


def rows(idx, k):
    return np.tile(idx, (k, 1))


def look(tab, idx):
    return np.take_along_axis(f64(tab), rows(idx, len(tab)), axis=1)


K, S, V, N = 128, 2048, 1536, 1536


def setup_inputs():
    return {"tab": f32(np.random.standard_normal((2, K, S))), "offs": striped(np.random.permutation(S)[:N])}


def reference(tab, offs):
    idx = offs[:16].T.reshape(-1)
    x = (np.minimum(np.maximum(look(tab[0], idx), -1.25), 1.0)) * (np.tanh(look(tab[1], idx)))
    return x

@@ -1,0 +1,35 @@
+import concourse.mybir as mybir
+
+F32, U16 = mybir.dt.float32, mybir.dt.uint16
+ALU = mybir.AluOpType
+TANH = mybir.ActivationFunctionType.Tanh
+
+LOW, HIGH = -1.25, 1.0
+ENTRIES_PER_COLUMN = 16
+PIECE = 512
+
+
+def tile_lookup_vg_cliptanh_out_kernel(tc, tab, offs, out):
+    nc = tc.nc
+    rows, places = tab.shape[1], tab.shape[2]
+    entries = out.shape[1]
+    pieces = entries // PIECE
+
+    with tc.tile_pool(name="held", bufs=1) as held, tc.tile_pool(name="work", bufs=pieces) as work:
+        offsets = held.tile([rows, entries // ENTRIES_PER_COLUMN], U16)
+        values = held.tile([rows, places], F32)
+        gates = held.tile([rows, places], F32)
+        nc.sync.dma_start(offsets[:], offs)
+        nc.sync.dma_start(values[:], tab[0])
+        nc.sync.dma_start(gates[:], tab[1])
+
+        for piece in range(pieces):
+            start, stop = piece * PIECE, (piece + 1) * PIECE
+            picks = offsets[:, start // ENTRIES_PER_COLUMN : stop // ENTRIES_PER_COLUMN]
+            clamped = work.tile([rows, PIECE], F32)
+            squashed = work.tile([rows, PIECE], F32)
+            product = work.tile([rows, PIECE], F32)
+            nc.vector.tensor_scalar(clamped[:], values[:].indirect(picks), LOW, HIGH, ALU.max, ALU.min)
+            nc.scalar.activation(squashed[:], gates[:].indirect(picks), TANH)
+            nc.vector.tensor_tensor(product[:], clamped[:], squashed[:], ALU.mult)
+            nc.sync.dma_start(out[:, start:stop], product[:])

@@ -6,30 +6,42 @@ TANH = mybir.ActivationFunctionType.Tanh
 
 LOW, HIGH = -1.25, 1.0
 ENTRIES_PER_COLUMN = 16
-PIECE = 512
+VALUE_PIECE = 768
+GATE_PIECE = 256
 
 
 def tile_lookup_vg_cliptanh_out_kernel(tc, tab, offs, out):
     nc = tc.nc
     rows, places = tab.shape[1], tab.shape[2]
     entries = out.shape[1]
-    pieces = entries // PIECE
 
-    with tc.tile_pool(name="held", bufs=1) as held, tc.tile_pool(name="work", bufs=pieces) as work:
+    with tc.tile_pool(name="held", bufs=1) as held:
         offsets = held.tile([rows, entries // ENTRIES_PER_COLUMN], U16)
         values = held.tile([rows, places], F32)
         gates = held.tile([rows, places], F32)
+        clamped = held.tile([rows, entries], F32)
+        squashed = held.tile([rows, entries], F32)
+        product = held.tile([rows, entries], F32)
+
+        def listed(start, stop):
+            return offsets[:, start // ENTRIES_PER_COLUMN : stop // ENTRIES_PER_COLUMN]
+
         nc.sync.dma_start(offsets[:], offs)
         nc.sync.dma_start(values[:], tab[0])
         nc.sync.dma_start(gates[:], tab[1])
 
-        for piece in range(pieces):
-            start, stop = piece * PIECE, (piece + 1) * PIECE
-            picks = offsets[:, start // ENTRIES_PER_COLUMN : stop // ENTRIES_PER_COLUMN]
-            clamped = work.tile([rows, PIECE], F32)
-            squashed = work.tile([rows, PIECE], F32)
-            product = work.tile([rows, PIECE], F32)
-            nc.vector.tensor_scalar(clamped[:], values[:].indirect(picks), LOW, HIGH, ALU.max, ALU.min)
-            nc.scalar.activation(squashed[:], gates[:].indirect(picks), TANH)
-            nc.vector.tensor_tensor(product[:], clamped[:], squashed[:], ALU.mult)
-            nc.sync.dma_start(out[:, start:stop], product[:])
+        zero = held.tile([rows, 1], F32)
+        warm = held.tile([rows, 1], F32)
+        nc.vector.memset(zero[:], 0.0)
+        nc.scalar.activation(warm[:], zero[:], TANH)
+
+        for start in range(0, entries, VALUE_PIECE):
+            stop = start + VALUE_PIECE
+            looked_up = values[:].indirect(listed(start, stop))
+            nc.vector.tensor_scalar(clamped[:, start:stop], looked_up, LOW, HIGH, ALU.max, ALU.min)
+
+        for start in range(0, entries, GATE_PIECE):
+            stop = start + GATE_PIECE
+            nc.scalar.activation(squashed[:, start:stop], gates[:].indirect(listed(start, stop)), TANH)
+            nc.vector.tensor_tensor(product[:, start:stop], clamped[:, start:stop], squashed[:, start:stop], ALU.mult)
+            nc.sync.dma_start(out[:, start:stop], product[:, start:stop])

@@ -1,3 +1,5 @@
+import itertools
+
 import concourse.mybir as mybir
 
 F32, U16 = mybir.dt.float32, mybir.dt.uint16
@@ -40,8 +42,10 @@ def tile_lookup_vg_cliptanh_out_kernel(tc, tab, offs, out):
             looked_up = values[:].indirect(listed(start, stop))
             nc.vector.tensor_scalar(clamped[:, start:stop], looked_up, LOW, HIGH, ALU.max, ALU.min)
 
-        for start in range(0, entries, GATE_PIECE):
-            stop = start + GATE_PIECE
+        middle = entries // GATE_PIECE - 3
+        widths = [2 * GATE_PIECE] + [GATE_PIECE] * middle + [GATE_PIECE // 2] * 2
+        for width, stop in zip(widths, itertools.accumulate(widths)):
+            start = stop - width
             nc.scalar.activation(squashed[:, start:stop], gates[:].indirect(listed(start, stop)), TANH)
             nc.vector.tensor_tensor(product[:, start:stop], clamped[:, start:stop], squashed[:, start:stop], ALU.mult)
             nc.sync.dma_start(out[:, start:stop], product[:, start:stop])

import itertools

import concourse.mybir as mybir

F32, U16 = mybir.dt.float32, mybir.dt.uint16
ALU = mybir.AluOpType
TANH = mybir.ActivationFunctionType.Tanh

LOW, HIGH = -1.25, 1.0
ENTRIES_PER_COLUMN = 16
VALUE_PIECE = 768
GATE_PIECE = 256


def tile_lookup_vg_cliptanh_out_kernel(tc, tab, offs, out):
    nc = tc.nc
    rows, places = tab.shape[1], tab.shape[2]
    entries = out.shape[1]

    with tc.tile_pool(name="held", bufs=1) as held:
        offsets = held.tile([rows, entries // ENTRIES_PER_COLUMN], U16)
        values = held.tile([rows, places], F32)
        gates = held.tile([rows, places], F32)
        clamped = held.tile([rows, entries], F32)
        squashed = held.tile([rows, entries], F32)
        product = held.tile([rows, entries], F32)

        def listed(start, stop):
            return offsets[:, start // ENTRIES_PER_COLUMN : stop // ENTRIES_PER_COLUMN]

        nc.sync.dma_start(offsets[:], offs)
        nc.sync.dma_start(values[:], tab[0])
        nc.sync.dma_start(gates[:], tab[1])

        zero = held.tile([rows, 1], F32)
        warm = held.tile([rows, 1], F32)
        nc.vector.memset(zero[:], 0.0)
        nc.scalar.activation(warm[:], zero[:], TANH)

        for start in range(0, entries, VALUE_PIECE):
            stop = start + VALUE_PIECE
            looked_up = values[:].indirect(listed(start, stop))
            nc.vector.tensor_scalar(clamped[:, start:stop], looked_up, LOW, HIGH, ALU.max, ALU.min)

        middle = entries // GATE_PIECE - 3
        widths = [2 * GATE_PIECE] + [GATE_PIECE] * middle + [GATE_PIECE // 2] * 2
        for width, stop in zip(widths, itertools.accumulate(widths)):
            start = stop - width
            nc.scalar.activation(squashed[:, start:stop], gates[:].indirect(listed(start, stop)), TANH)
            nc.vector.tensor_tensor(product[:, start:stop], clamped[:, start:stop], squashed[:, start:stop], ALU.mult)
            nc.sync.dma_start(out[:, start:stop], product[:, start:stop])
